import numpy as np
import ml_dtypes


def mxq(x, axis, fmt="e4m3"):
    dtype, down = {"e4m3": (ml_dtypes.float8_e4m3fn, 7), "e5m2": (ml_dtypes.float8_e5m2, 14)}[fmt]
    v = np.moveaxis(np.asarray(x, np.float32).astype(ml_dtypes.bfloat16).astype(np.float64), axis, -1)
    blocks = v.reshape(v.shape[:-1] + (-1, 32))
    amax = np.abs(blocks).max(-1, keepdims=True)
    byte = np.maximum(np.where(amax > 0, np.frexp(amax)[1] - 1 + 127, 0) - down, 1)
    scale = np.exp2(byte - 127.0)
    codes = (blocks / scale).astype(np.float32).astype(dtype).astype(np.float64)
    return np.moveaxis((codes * scale).reshape(v.shape), -1, axis)


WIDE = False


def mx_kscale(k):
    if not WIDE:
        return np.ones(k)
    levels = np.array([10, -10, 5, -5, 0])
    if k % 512:
        return np.exp2(np.random.permutation(np.resize(levels, k // 32))).repeat(32)
    a = np.empty((k // 512, 16))
    for p in range(k // 512):
        a[p, :8] = np.random.permutation(np.resize(levels, 8))
        for g in range(8):
            far = levels[np.abs(levels - a[p, g]) >= 10]
            a[p, g + 8] = far[np.random.randint(len(far))]
    return np.exp2(a.ravel()).repeat(32)


def f64(x):
    return np.asarray(x).astype(np.float64)


def striped(idx):
    return np.tile(np.asarray(idx).reshape(-1, 16).T, (8, 1)).astype(np.uint16)


def unstriped(offs):
    return offs[:16].T.reshape(-1).astype(np.int64)


E2M1 = np.array([0.0, 0.5, 1.0, 1.5, 2.0, 3.0, 4.0, 6.0, -0.0, -0.5, -1.0, -1.5, -2.0, -3.0, -4.0, -6.0])


def pack_weight(w, fmt):
    k, n = w.shape
    w = f64(np.asarray(w, np.float32).astype(ml_dtypes.bfloat16)).reshape(k // 32, 32, n)
    amax = np.abs(w).max(1)
    if fmt == "e4m3":
        byte = np.frexp(amax)[1] - 1 + 127 - 7
    else:
        mant, ex = np.frexp(amax / 6.0)
        byte = np.where(mant > 0.5, ex, ex - 1) + 127
    byte = np.clip(np.where(amax > 0, byte, 1), 1, 254)
    scaled = (w * np.exp2(127.0 - byte)[:, None, :]).reshape(k, n).astype(np.float32)
    by_word = np.ascontiguousarray(scaled.reshape(k // 512, 128, 4, n).transpose(0, 1, 3, 2))
    if fmt == "e4m3":
        words = by_word.astype(ml_dtypes.float8_e4m3fn).view(np.uint8)
    else:
        c = by_word.astype(ml_dtypes.float4_e2m1fn).view(np.uint8) & 0xF
        words = (c[..., 0::2] | (c[..., 1::2] << 4)).reshape(k // 512, 128, 2 * n)
    return np.ascontiguousarray(words), np.ascontiguousarray(byte.astype(np.uint8).reshape(k // 512, 16, n))


def unpack_weight(words, scales, fmt):
    g, _, n = scales.shape
    words = np.ascontiguousarray(words).reshape(g, 128, n, -1)
    if fmt == "e4m3":
        vals = words.view(ml_dtypes.float8_e4m3fn).astype(np.float64)
    else:
        nib = np.empty((g, 128, n, 4), np.uint8)
        nib[..., 0::2] = words & 0xF
        nib[..., 1::2] = words >> 4
        vals = E2M1[nib]
    vals = vals * np.repeat(np.exp2(scales.astype(np.float64) - 127.0), 8, axis=1)[..., None]
    return vals.transpose(0, 1, 3, 2).reshape(g * 512, n)


D, T, U, I, J, G = 512, 1024, 1024, 256, 512, 64


def setup_inputs():
    n = np.random.standard_normal
    idx = np.random.permutation(T)[:I]
    idx2 = np.random.permutation(U)[:J]
    fd = mx_kscale(D)
    tabbp = pack_weight(n((D, U)) / fd[:, None], "e4m3")
    return {
        "taba": (n((D, T)) * 1 / np.sqrt(D) * fd[:, None]).astype(np.float32),
        "tabb_words": tabbp[0],
        "tabb_scales": tabbp[1],
        "val": (np.random.uniform(-1.5, 1.5, (1, J))).astype(np.float32),
        "aim": (n((I, G)) * 1.0).astype(np.float32),
        "old": (0.3 * n((I, J))).astype(np.float32),
        "offs": striped(idx),
        "offs2": striped(idx2),
    }


def reference(taba, tabb_words, tabb_scales, val, aim, old, offs, offs2):
    idx = unstriped(offs)
    idx2 = unstriped(offs2)
    tabbu = unpack_weight(tabb_words, tabb_scales, "e4m3")
    tabaidxq = mxq(f64(taba)[:, idx], 0, "e4m3")
    tabbidx2g = tabbu[:, idx2]
    s = tabaidxq.T @ tabbidx2g
    p = np.exp(s)
    z = p.reshape(I, G, J // G).sum(axis=2)
    ev = (p * f64(val)).reshape(I, G, J // G).sum(axis=2) / z
    dev = (ev - f64(aim)) * 2.0
    e1 = dev / z
    r1 = np.repeat(e1, J // G, axis=1)
    dz = dev * (p * f64(val)).reshape(I, G, J // G).sum(axis=2) / np.square(z) * (-1.0)
    r2 = np.repeat(dz, J // G, axis=1)
    dp = r1 * f64(val) + r2
    ds = dp * p
    y = ds * 4.0 + f64(old)
    return y

@@ -1,0 +1,188 @@
+from contextlib import ExitStack
+
+import concourse.mybir as mybir
+from concourse.masks import make_identity
+
+D, T, U, I, J, G = 512, 1024, 1024, 256, 512, 64
+FLOPS = 2 * D * I * J
+
+F32 = mybir.dt.float32
+BF16 = mybir.dt.bfloat16
+I32 = mybir.dt.int32
+U32 = mybir.dt.uint32
+U16 = mybir.dt.uint16
+U8 = mybir.dt.uint8
+FP8X4 = mybir.dt.float8_e4m3fn_x4
+ALU = mybir.AluOpType
+ACT = mybir.ActivationFunctionType
+AX = mybir.AxisListType
+
+P = 128
+PACK = 4
+MEMBERS = J // G
+ROW_TILES = I // P
+HALF = J // 2
+HALF_GROUPS = G // 2
+
+
+def tile_attend_bexpectedvalue_kernel(tc, taba, tabb_words, tabb_scales, val, aim, old, offs, offs2, out):
+    nc = tc.nc
+    with ExitStack() as ctx:
+        keep = ctx.enter_context(tc.tile_pool(name="keep", bufs=1))
+        psum = ctx.enter_context(tc.psum_pool(name="psum", bufs=1))
+        hop = ctx.enter_context(tc.psum_pool(name="hop", bufs=2))
+
+        list_a = keep.tile([P, I // 16], U16, name="list_a")
+        list_b = keep.tile([P, J // 16], U16, name="list_b")
+        nc.sync.dma_start(list_b[:], offs2)
+        nc.sync.dma_start(list_a[:], offs)
+
+        b_scale_all = keep.tile([P, U], U8, name="b_scale_all", align_bytes=64)
+        nc.vector.memset(b_scale_all[:].bitcast(I32), 0)
+        for q in range(4):
+            nc.scalar.dma_start(
+                b_scale_all[32 * q : 32 * q + 4, :].bitcast(I32),
+                tabb_scales[0, 4 * q : 4 * q + 4, :].bitcast(I32),
+            )
+
+        a_rows = taba.rearrange("(p t) c -> p t c", t=PACK)
+        a_planes = []
+        for t in range(PACK):
+            plane = keep.tile([P, T], F32, name=f"a_plane{t}")
+            nc.sync.dma_start(plane[:], a_rows[:, t, :])
+            a_planes.append(plane)
+        b_word_all = keep.tile([P, U], U32, name="b_word_all")
+        nc.sync.dma_start(
+            b_word_all[:].bitcast(I32),
+            tabb_words[0].rearrange("p c r -> p (c r)").bitcast(I32),
+        )
+        val_cols = keep.tile([P, PACK], F32, name="val_cols")
+        nc.sync.dma_start(val_cols[:], val.rearrange("o (p t) -> (o p) t", t=PACK))
+        aim_sb = keep.tile([P, ROW_TILES, G], F32, name="aim_sb")
+        nc.sync.dma_start(aim_sb[:], aim.rearrange("(r p) g -> p r g", p=P))
+        old_sb = keep.tile([P, ROW_TILES, J], F32, name="old_sb")
+        nc.sync.dma_start(old_sb[:], old.rearrange("(r p) j -> p r j", p=P))
+
+        ident = keep.tile([P, P], F32, name="ident")
+        make_identity(nc, ident[:])
+
+        warm = keep.tile([P, 1], F32, name="warm")
+        nc.scalar.activation(warm[:], ident[:, 0:1], ACT.Exp)
+
+        val_ps = psum.tile([P, PACK, P], F32, name="val_ps")
+        for t in range(PACK):
+            nc.tensor.transpose(val_ps[:, t, :], val_cols[:, t : t + 1].to_broadcast([P, P]), ident[:])
+        val_row = keep.tile([P, J], F32, name="val_row")
+        nc.scalar.copy(val_row[:].rearrange("x (p t) -> x p t", t=PACK), val_ps[:].rearrange("x t p -> x p t"))
+
+        b_scale = keep.tile([P, J], U8, name="b_scale", align_bytes=64)
+        nc.vector.tensor_copy(b_scale[:], b_scale_all[:].indirect(list_b[:]))
+
+        a_grouped = keep.tile([P, I, PACK], BF16, name="a_grouped", align_bytes=64)
+        for t in range(PACK):
+            nc.vector.tensor_copy(a_grouped[:, :, t], a_planes[t][:].indirect(list_a[:]))
+        a_codes = keep.tile([P, I], U32, name="a_codes", align_bytes=64)
+        a_scale = keep.tile([P, I], U8, name="a_scale", align_bytes=64)
+        nc.vector.quantize_mx(
+            out=a_codes[:].bitcast(FP8X4), scales=a_scale[:], in_=a_grouped[:].rearrange("p i t -> p (i t)")
+        )
+
+        scores = []
+        for h in range(2):
+            b_words = keep.tile([P, HALF], U32, name=f"b_words{h}", align_bytes=64)
+            nc.vector.tensor_copy(
+                b_words[:], b_word_all[:].indirect(list_b[:, h * (HALF // 16) : (h + 1) * (HALF // 16)])
+            )
+            bank = psum.tile([P, ROW_TILES, HALF], F32, name=f"score{h}")
+            for r in range(ROW_TILES):
+                rows = slice(r * P, (r + 1) * P)
+                nc.tensor.matmul_mx(
+                    out=bank[:, r, :],
+                    lhsT=a_codes[:, rows].bitcast(FP8X4),
+                    lhsT_scale=a_scale[:, rows],
+                    rhs=b_words[:].bitcast(FP8X4),
+                    rhs_scale=b_scale[:, h * HALF : (h + 1) * HALF],
+                    start=True,
+                    stop=True,
+                )
+            scores.append(bank)
+
+        def by_group(ap):
+            return ap.rearrange("p r (g k) -> p (r g) k", k=MEMBERS)
+
+        def spread(ap):
+            return ap.unsqueeze(2).to_broadcast([P, ap.shape[1], MEMBERS])
+
+        for h in range(2):
+            cols = slice(h * HALF, (h + 1) * HALF)
+            s = by_group(scores[h][:])
+            neg_max = keep.tile([P, G], F32, name=f"neg_max{h}")
+            nc.vector.tensor_reduce(neg_max[:], s, AX.X, ALU.max, negate=True)
+            shifted = keep.tile([P, ROW_TILES, HALF], F32, name=f"shifted{h}")
+            nc.vector.tensor_tensor(by_group(shifted[:]), s, spread(neg_max[:]), ALU.add)
+            p = keep.tile([P, ROW_TILES, HALF], F32, name=f"p{h}")
+            nc.scalar.activation(p[:], shifted[:], ACT.Exp)
+            z = keep.tile([P, G], F32, name=f"z{h}")
+            nc.vector.tensor_reduce(z[:], by_group(p[:]), AX.X, ALU.add)
+            pv = keep.tile([P, ROW_TILES, HALF], F32, name=f"pv{h}")
+            nc.vector.tensor_tensor(
+                pv[:], p[:], val_row[:, cols].unsqueeze(1).to_broadcast([P, ROW_TILES, HALF]), ALU.mult
+            )
+            rz = keep.tile([P, G], F32, name=f"rz{h}")
+            nc.vector.reciprocal(rz[:], z[:])
+            n = keep.tile([P, G], F32, name=f"n{h}")
+            nc.vector.tensor_reduce(n[:], by_group(pv[:]), AX.X, ALU.add)
+            ev = keep.tile([P, G], F32, name=f"ev{h}")
+            nc.vector.tensor_tensor(ev[:], n[:], rz[:], ALU.mult)
+            dev = keep.tile([P, G], F32, name=f"dev{h}")
+            nc.vector.tensor_tensor(
+                dev[:].rearrange("p (r g) -> p r g", r=ROW_TILES),
+                ev[:].rearrange("p (r g) -> p r g", r=ROW_TILES),
+                aim_sb[:, :, h * HALF_GROUPS : (h + 1) * HALF_GROUPS],
+                ALU.subtract,
+            )
+            ev_rz = keep.tile([P, G], F32, name=f"ev_rz{h}")
+            nc.vector.scalar_tensor_tensor(ev_rz[:], ev[:], -8.0, rz[:], ALU.mult, ALU.mult)
+            c = keep.tile([P, G], F32, name=f"c{h}")
+            nc.vector.scalar_tensor_tensor(c[:], dev[:], 8.0, rz[:], ALU.mult, ALU.mult)
+            d = keep.tile([P, G], F32, name=f"d{h}")
+            nc.vector.tensor_tensor(d[:], dev[:], ev_rz[:], ALU.mult)
+
+            for r in range(ROW_TILES):
+                groups = slice(r * HALF_GROUPS, (r + 1) * HALF_GROUPS)
+                a = keep.tile([P, HALF], F32, name=f"a{h}{r}")
+                b = keep.tile([P, HALF], F32, name=f"b{h}{r}")
+                nc.vector.tensor_tensor(
+                    a[:].rearrange("p (g k) -> p g k", k=MEMBERS),
+                    pv[:, r, :].rearrange("p (g k) -> p g k", k=MEMBERS),
+                    spread(c[:, groups]),
+                    ALU.mult,
+                )
+                nc.vector.tensor_tensor(
+                    b[:].rearrange("p (g k) -> p g k", k=MEMBERS),
+                    p[:, r, :].rearrange("p (g k) -> p g k", k=MEMBERS),
+                    spread(d[:, groups]),
+                    ALU.mult,
+                )
+                result = keep.tile([P, HALF], F32, name=f"result{h}{r}")
+                if h == 1:
+                    ab = keep.tile([P, HALF], F32, name=f"ab{r}")
+                    nc.vector.tensor_tensor(ab[:], a[:], old_sb[:, r, cols], ALU.add)
+                    nc.vector.tensor_tensor(result[:], ab[:], b[:], ALU.add)
+                else:
+                    turned_ps = hop.tile([P, HALF], F32, name="turned_ps")
+                    for k in range(HALF // P):
+                        blk = slice(k * P, (k + 1) * P)
+                        terms = (old_sb[:, r, h * HALF + k * P : h * HALF + (k + 1) * P], a[:, blk], b[:, blk])
+                        for m, term in enumerate(terms):
+                            nc.tensor.matmul(
+                                turned_ps[:, blk], term, ident[:], start=(m == 0), stop=(m == 2), is_transpose=True
+                            )
+                    turned = keep.tile([P, HALF], F32, name=f"turned{h}{r}")
+                    nc.scalar.copy(turned[:], turned_ps[:])
+                    back_ps = hop.tile([P, HALF], F32, name="back_ps")
+                    for k in range(HALF // P):
+                        blk = slice(k * P, (k + 1) * P)
+                        nc.tensor.transpose(back_ps[:, blk], turned[:, blk], ident[:])
+                    nc.scalar.copy(result[:], back_ps[:])
+                nc.sync.dma_start(out[r * P : (r + 1) * P, cols], result[:])

@@ -23,6 +23,8 @@ MEMBERS = J // G
 ROW_TILES = I // P
 HALF = J // 2
 HALF_GROUPS = G // 2
+WIDE = ROW_TILES * HALF
+BLOCKS = WIDE // P
 
 
 def tile_attend_bexpectedvalue_kernel(tc, taba, tabb_words, tabb_scales, val, aim, old, offs, offs2, out):
@@ -30,15 +32,19 @@ def tile_attend_bexpectedvalue_kernel(tc, taba, tabb_words, tabb_scales, val, ai
     with ExitStack() as ctx:
         keep = ctx.enter_context(tc.tile_pool(name="keep", bufs=1))
         psum = ctx.enter_context(tc.psum_pool(name="psum", bufs=1))
-        hop = ctx.enter_context(tc.psum_pool(name="hop", bufs=2))
+
+        def bank(tag, name):
+            return psum.tile([P, WIDE], F32, name=name, tag=tag)
 
         list_a = keep.tile([P, I // 16], U16, name="list_a")
         list_b = keep.tile([P, J // 16], U16, name="list_b")
         nc.sync.dma_start(list_b[:], offs2)
         nc.sync.dma_start(list_a[:], offs)
 
+        val_cols = keep.tile([P, PACK], F32, name="val_cols")
+        nc.scalar.dma_start(val_cols[:], val.rearrange("o (p t) -> (o p) t", t=PACK))
         b_scale_all = keep.tile([P, U], U8, name="b_scale_all", align_bytes=64)
-        nc.vector.memset(b_scale_all[:].bitcast(I32), 0)
+        nc.gpsimd.memset(b_scale_all[:].bitcast(I32), 0)
         for q in range(4):
             nc.scalar.dma_start(
                 b_scale_all[32 * q : 32 * q + 4, :].bitcast(I32),
@@ -56,8 +62,6 @@ def tile_attend_bexpectedvalue_kernel(tc, taba, tabb_words, tabb_scales, val, ai
             b_word_all[:].bitcast(I32),
             tabb_words[0].rearrange("p c r -> p (c r)").bitcast(I32),
         )
-        val_cols = keep.tile([P, PACK], F32, name="val_cols")
-        nc.sync.dma_start(val_cols[:], val.rearrange("o (p t) -> (o p) t", t=PACK))
         aim_sb = keep.tile([P, ROW_TILES, G], F32, name="aim_sb")
         nc.sync.dma_start(aim_sb[:], aim.rearrange("(r p) g -> p r g", p=P))
         old_sb = keep.tile([P, ROW_TILES, J], F32, name="old_sb")
@@ -69,120 +73,211 @@ def tile_attend_bexpectedvalue_kernel(tc, taba, tabb_words, tabb_scales, val, ai
         warm = keep.tile([P, 1], F32, name="warm")
         nc.scalar.activation(warm[:], ident[:, 0:1], ACT.Exp)
 
-        val_ps = psum.tile([P, PACK, P], F32, name="val_ps")
+        def turn(dst, src, start=True, stop=True):
+            nc.tensor.matmul(dst, src, ident[:], start=start, stop=stop, is_transpose=True)
+
+        def block(ap, q):
+            return ap[:, q * P : (q + 1) * P]
+
+        val_ps = bank("turn", "val_ps")
         for t in range(PACK):
-            nc.tensor.transpose(val_ps[:, t, :], val_cols[:, t : t + 1].to_broadcast([P, P]), ident[:])
-        val_row = keep.tile([P, J], F32, name="val_row")
-        nc.scalar.copy(val_row[:].rearrange("x (p t) -> x p t", t=PACK), val_ps[:].rearrange("x t p -> x p t"))
+            turn(block(val_ps, t), val_cols[:, t : t + 1].to_broadcast([P, P]))
+        val_tp = val_ps[:].rearrange("x (t p) -> x t p", t=PACK)
+        val_row = keep.tile([P, HALF], F32, name="val_row")
+        nc.scalar.copy(
+            val_row[:].rearrange("x (p t) -> x p t", t=PACK), val_tp[:, :, 0 : P // 2].rearrange("x t p -> x p t")
+        )
+        val_dealt = keep.tile([P, WIDE], F32, name="val_dealt", tag="ahead", align_bytes=64)
+        for r in range(ROW_TILES):
+            nc.scalar.copy(
+                val_dealt[:].rearrange("x (u t r g) -> x r u t g", u=2, t=PACK, r=ROW_TILES)[:, r],
+                val_tp[:, :, P // 2 : P].rearrange("x t (g u) -> x u t g", u=2),
+            )
+        val_ps2 = bank("back", "val_ps2")
+        for q in range(BLOCKS):
+            turn(block(val_ps2, q), block(val_dealt, q))
+        val_part = keep.tile([P, BLOCKS], F32, name="val_part")
+        nc.scalar.copy(val_part[:], val_ps2[:].rearrange("x (q c) -> x q c", q=BLOCKS)[:, :, 0])
 
         b_scale = keep.tile([P, J], U8, name="b_scale", align_bytes=64)
         nc.vector.tensor_copy(b_scale[:], b_scale_all[:].indirect(list_b[:]))
 
-        a_grouped = keep.tile([P, I, PACK], BF16, name="a_grouped", align_bytes=64)
+        a_grouped = keep.tile([P, I, PACK], BF16, name="a_grouped", tag="shared", align_bytes=64)
         for t in range(PACK):
             nc.vector.tensor_copy(a_grouped[:, :, t], a_planes[t][:].indirect(list_a[:]))
-        a_codes = keep.tile([P, I], U32, name="a_codes", align_bytes=64)
+        a_codes = keep.tile([P, I], U32, name="a_codes", tag="ahead", align_bytes=64)
         a_scale = keep.tile([P, I], U8, name="a_scale", align_bytes=64)
         nc.vector.quantize_mx(
             out=a_codes[:].bitcast(FP8X4), scales=a_scale[:], in_=a_grouped[:].rearrange("p i t -> p (i t)")
         )
 
-        scores = []
+        b_words = keep.tile([P, J], U32, name="b_words", tag="shared", align_bytes=64)
+        scores = {}
         for h in range(2):
-            b_words = keep.tile([P, HALF], U32, name=f"b_words{h}", align_bytes=64)
             nc.vector.tensor_copy(
-                b_words[:], b_word_all[:].indirect(list_b[:, h * (HALF // 16) : (h + 1) * (HALF // 16)])
+                b_words[:, h * HALF : (h + 1) * HALF],
+                b_word_all[:].indirect(list_b[:, h * (HALF // 16) : (h + 1) * (HALF // 16)]),
             )
-            bank = psum.tile([P, ROW_TILES, HALF], F32, name=f"score{h}")
             for r in range(ROW_TILES):
                 rows = slice(r * P, (r + 1) * P)
+                scores[h, r] = bank(f"score{h}{r}", f"score{h}{r}")[:, 0:HALF]
                 nc.tensor.matmul_mx(
-                    out=bank[:, r, :],
+                    out=scores[h, r],
                     lhsT=a_codes[:, rows].bitcast(FP8X4),
                     lhsT_scale=a_scale[:, rows],
-                    rhs=b_words[:].bitcast(FP8X4),
+                    rhs=b_words[:, h * HALF : (h + 1) * HALF].bitcast(FP8X4),
                     rhs_scale=b_scale[:, h * HALF : (h + 1) * HALF],
                     start=True,
                     stop=True,
                 )
-            scores.append(bank)
 
         def by_group(ap):
-            return ap.rearrange("p r (g k) -> p (r g) k", k=MEMBERS)
+            return ap.rearrange("p (g k) -> p g k", k=MEMBERS)
 
         def spread(ap):
             return ap.unsqueeze(2).to_broadcast([P, ap.shape[1], MEMBERS])
 
-        for h in range(2):
-            cols = slice(h * HALF, (h + 1) * HALF)
-            s = by_group(scores[h][:])
-            neg_max = keep.tile([P, G], F32, name=f"neg_max{h}")
-            nc.vector.tensor_reduce(neg_max[:], s, AX.X, ALU.max, negate=True)
-            shifted = keep.tile([P, ROW_TILES, HALF], F32, name=f"shifted{h}")
-            nc.vector.tensor_tensor(by_group(shifted[:]), s, spread(neg_max[:]), ALU.add)
-            p = keep.tile([P, ROW_TILES, HALF], F32, name=f"p{h}")
-            nc.scalar.activation(p[:], shifted[:], ACT.Exp)
-            z = keep.tile([P, G], F32, name=f"z{h}")
-            nc.vector.tensor_reduce(z[:], by_group(p[:]), AX.X, ALU.add)
-            pv = keep.tile([P, ROW_TILES, HALF], F32, name=f"pv{h}")
-            nc.vector.tensor_tensor(
-                pv[:], p[:], val_row[:, cols].unsqueeze(1).to_broadcast([P, ROW_TILES, HALF]), ALU.mult
-            )
-            rz = keep.tile([P, G], F32, name=f"rz{h}")
-            nc.vector.reciprocal(rz[:], z[:])
-            n = keep.tile([P, G], F32, name=f"n{h}")
-            nc.vector.tensor_reduce(n[:], by_group(pv[:]), AX.X, ALU.add)
-            ev = keep.tile([P, G], F32, name=f"ev{h}")
-            nc.vector.tensor_tensor(ev[:], n[:], rz[:], ALU.mult)
-            dev = keep.tile([P, G], F32, name=f"dev{h}")
-            nc.vector.tensor_tensor(
-                dev[:].rearrange("p (r g) -> p r g", r=ROW_TILES),
-                ev[:].rearrange("p (r g) -> p r g", r=ROW_TILES),
-                aim_sb[:, :, h * HALF_GROUPS : (h + 1) * HALF_GROUPS],
-                ALU.subtract,
-            )
-            ev_rz = keep.tile([P, G], F32, name=f"ev_rz{h}")
-            nc.vector.scalar_tensor_tensor(ev_rz[:], ev[:], -8.0, rz[:], ALU.mult, ALU.mult)
-            c = keep.tile([P, G], F32, name=f"c{h}")
-            nc.vector.scalar_tensor_tensor(c[:], dev[:], 8.0, rz[:], ALU.mult, ALU.mult)
-            d = keep.tile([P, G], F32, name=f"d{h}")
-            nc.vector.tensor_tensor(d[:], dev[:], ev_rz[:], ALU.mult)
+        def small(name):
+            return keep.tile([P, G], F32, name=name)
 
-            for r in range(ROW_TILES):
-                groups = slice(r * HALF_GROUPS, (r + 1) * HALF_GROUPS)
-                a = keep.tile([P, HALF], F32, name=f"a{h}{r}")
-                b = keep.tile([P, HALF], F32, name=f"b{h}{r}")
-                nc.vector.tensor_tensor(
-                    a[:].rearrange("p (g k) -> p g k", k=MEMBERS),
-                    pv[:, r, :].rearrange("p (g k) -> p g k", k=MEMBERS),
-                    spread(c[:, groups]),
-                    ALU.mult,
-                )
-                nc.vector.tensor_tensor(
-                    b[:].rearrange("p (g k) -> p g k", k=MEMBERS),
-                    p[:, r, :].rearrange("p (g k) -> p g k", k=MEMBERS),
-                    spread(d[:, groups]),
-                    ALU.mult,
-                )
-                result = keep.tile([P, HALF], F32, name=f"result{h}{r}")
-                if h == 1:
-                    ab = keep.tile([P, HALF], F32, name=f"ab{r}")
-                    nc.vector.tensor_tensor(ab[:], a[:], old_sb[:, r, cols], ALU.add)
-                    nc.vector.tensor_tensor(result[:], ab[:], b[:], ALU.add)
-                else:
-                    turned_ps = hop.tile([P, HALF], F32, name="turned_ps")
-                    for k in range(HALF // P):
-                        blk = slice(k * P, (k + 1) * P)
-                        terms = (old_sb[:, r, h * HALF + k * P : h * HALF + (k + 1) * P], a[:, blk], b[:, blk])
-                        for m, term in enumerate(terms):
-                            nc.tensor.matmul(
-                                turned_ps[:, blk], term, ident[:], start=(m == 0), stop=(m == 2), is_transpose=True
-                            )
-                    turned = keep.tile([P, HALF], F32, name=f"turned{h}{r}")
-                    nc.scalar.copy(turned[:], turned_ps[:])
-                    back_ps = hop.tile([P, HALF], F32, name="back_ps")
-                    for k in range(HALF // P):
-                        blk = slice(k * P, (k + 1) * P)
-                        nc.tensor.transpose(back_ps[:, blk], turned[:, blk], ident[:])
-                    nc.scalar.copy(result[:], back_ps[:])
-                nc.sync.dma_start(out[r * P : (r + 1) * P, cols], result[:])
+        def wide(name):
+            return keep.tile([P, WIDE], F32, name=name)
+
+        def by_row_tile(ap):
+            return ap.rearrange("p (r g) -> p r g", r=ROW_TILES)
+
+        groups = [slice(r * HALF_GROUPS, (r + 1) * HALF_GROUPS) for r in range(ROW_TILES)]
+        cols = [slice(r * HALF, (r + 1) * HALF) for r in range(ROW_TILES)]
+
+        neg_max0 = small("neg_max0")
+        neg_max1 = small("neg_max1")
+        shifted0 = wide("shifted0")
+        p0 = wide("p0")
+        pv0 = wide("pv0")
+        dealt1 = wide("dealt1")
+        for r in range(ROW_TILES):
+            nc.vector.tensor_reduce(neg_max0[:, groups[r]], by_group(scores[0, r]), AX.X, ALU.max, negate=True)
+        for r in range(ROW_TILES):
+            nc.vector.tensor_tensor(
+                by_group(shifted0[:, cols[r]]), by_group(scores[0, r]), spread(neg_max0[:, groups[r]]), ALU.add
+            )
+            nc.scalar.copy(
+                dealt1[:].rearrange("p (k g) -> p k g", k=MEMBERS)[:, :, groups[r]],
+                scores[1, r].rearrange("p (g k) -> p k g", k=MEMBERS),
+            )
+            nc.scalar.activation(p0[:, cols[r]], shifted0[:, cols[r]], ACT.Exp)
+            nc.gpsimd.tensor_tensor(pv0[:, cols[r]], p0[:, cols[r]], val_row[:], ALU.mult)
+        for r in range(ROW_TILES):
+            nc.vector.tensor_reduce(neg_max1[:, groups[r]], by_group(scores[1, r]), AX.X, ALU.max, negate=True)
+        neg_max_twice = keep.tile([P, 2, G], F32, name="neg_max_twice")
+        nc.scalar.copy(neg_max_twice[:], neg_max1[:].unsqueeze(1).to_broadcast([P, 2, G]))
+
+        turned_ps = bank("turn", "turned_ps")
+        for q in range(BLOCKS):
+            turn(block(turned_ps, q), block(dealt1, q), start=(q == 0), stop=False)
+        for q in range(BLOCKS):
+            turn(
+                block(turned_ps, q),
+                neg_max_twice[:].rearrange("p k g -> p (k g)"),
+                start=False,
+                stop=(q == BLOCKS - 1),
+            )
+        p_turned = wide("p_turned")
+        nc.scalar.activation(p_turned[:], turned_ps[:], ACT.Exp)
+        pv_turned = wide("pv_turned")
+        for q in range(BLOCKS):
+            nc.scalar.activation(block(pv_turned, q), block(p_turned, q), ACT.Copy, scale=val_part[:, q : q + 1])
+        z_ps = bank("score10", "z_ps")
+        for q in range(BLOCKS):
+            turn(block(z_ps, 0), block(p_turned, q), start=(q == 0), stop=(q == BLOCKS - 1))
+        n_ps = bank("score11", "n_ps")
+        for q in range(BLOCKS):
+            turn(block(n_ps, 0), block(pv_turned, q), start=(q == 0), stop=(q == BLOCKS - 1))
+        pv1 = bank("pv1", "pv1")
+        for q in range(BLOCKS):
+            turn(block(pv1, q), block(pv_turned, q))
+        p1 = bank("p1", "p1")
+        for q in range(BLOCKS):
+            turn(block(p1, q), block(p_turned, q))
+
+        z0 = small("z0")
+        rz0 = small("rz0")
+        n0 = small("n0")
+        for r in range(ROW_TILES):
+            nc.vector.tensor_reduce(z0[:, groups[r]], by_group(p0[:, cols[r]]), AX.X, ALU.add)
+        for r in range(ROW_TILES):
+            nc.vector.reciprocal(rz0[:, groups[r]], z0[:, groups[r]])
+        for r in range(ROW_TILES):
+            nc.vector.tensor_reduce(n0[:, groups[r]], by_group(pv0[:, cols[r]]), AX.X, ALU.add)
+
+        def pair_sum(dst, src_ps):
+            nc.vector.tensor_reduce(dst, block(src_ps, 0).rearrange("p (k g) -> p g k", k=2), AX.X, ALU.add)
+
+        def deviation(h, n, rz):
+            ev = small(f"ev{h}")
+            nc.vector.tensor_tensor(ev[:], n, rz, ALU.mult)
+            dev = small(f"dev{h}")
+            nc.vector.tensor_tensor(by_row_tile(dev[:]), by_row_tile(ev[:]), aim_sb[:, :, groups[h]], ALU.subtract)
+            return ev, dev
+
+        def factors(h, c, ev, dev, rz):
+            nc.vector.scalar_tensor_tensor(c, dev[:], 8.0, rz, ALU.mult, ALU.mult)
+            d = small(f"d{h}")
+            nc.vector.scalar_tensor_tensor(d[:], c, -1.0, ev[:], ALU.mult, ALU.mult)
+            return d
+
+        ev0, dev0 = deviation(0, n0[:], rz0[:])
+        z1 = n0
+        pair_sum(z1[:], z_ps)
+        rz1 = small("rz1")
+        nc.vector.reciprocal(rz1[:], z1[:])
+        overlap = keep.tile([P, G + HALF_GROUPS], F32, name="overlap")
+        c0 = overlap[:, HALF_GROUPS : HALF_GROUPS + G]
+        n1 = overlap[:, 0:G]
+        d0 = factors(0, c0, ev0, dev0, rz0[:])
+
+        def finish_first_half(r):
+            a = keep.tile([P, HALF], F32, name=f"a0{r}")
+            b = keep.tile([P, HALF], F32, name=f"b0{r}")
+            nc.vector.tensor_tensor(by_group(a[:]), by_group(pv0[:, cols[r]]), spread(c0[:, groups[r]]), ALU.mult)
+            nc.vector.tensor_tensor(by_group(b[:]), by_group(p0[:, cols[r]]), spread(d0[:, groups[r]]), ALU.mult)
+            sum_ps = bank(f"score0{r}", f"sum_ps{r}")
+            terms = (old_sb[:, r, 0:HALF], a[:], b[:])
+            for m, term in enumerate(terms):
+                for k in range(HALF // P):
+                    turn(block(sum_ps, k), block(term, k), start=(m == 0 and k == 0), stop=(m == 2 and k == 1))
+            sum_turned = keep.tile([P, HALF], F32, name=f"sum_turned{r}")
+            nc.scalar.copy(sum_turned[:], sum_ps[:, 0:HALF])
+            back_ps = bank(("turn", "back")[r], f"back_ps{r}")
+            for k in range(HALF // P):
+                turn(block(back_ps, k), block(sum_turned, k))
+            result = keep.tile([P, HALF], F32, name=f"result0{r}")
+            nc.scalar.copy(result[:], back_ps[:, 0:HALF])
+            nc.scalar.dma_start(out[r * P : (r + 1) * P, 0:HALF], result[:])
+
+        finish_first_half(0)
+        pair_sum(n1, n_ps)
+        ev1, dev1 = deviation(1, n1, rz1[:])
+        c1 = small("c1")
+        d1 = factors(1, c1[:], ev1, dev1, rz1[:])
+        finish_first_half(1)
+
+        a1 = wide("a1")
+        for r in range(ROW_TILES):
+            nc.vector.tensor_tensor(
+                by_group(a1[:, cols[r]]),
+                pv1[:].rearrange("p (k g) -> p g k", k=MEMBERS)[:, groups[r], :],
+                spread(c1[:, groups[r]]),
+                ALU.mult,
+            )
+        b1 = wide("b1")
+        nc.vector.tensor_tensor(
+            by_group(b1[:]), p1[:].rearrange("p (k g) -> p g k", k=MEMBERS), spread(d1[:]), ALU.mult
+        )
+        partial = [keep.tile([P, HALF], F32, name=f"partial{r}") for r in range(ROW_TILES)]
+        for r in range(ROW_TILES):
+            (nc.gpsimd, nc.vector)[r].tensor_tensor(partial[r][:], a1[:, cols[r]], old_sb[:, r, HALF:J], ALU.add)
+        for r in range(ROW_TILES):
+            result = keep.tile([P, HALF], F32, name=f"result1{r}")
+            nc.vector.tensor_tensor(result[:], partial[r][:], b1[:, cols[r]], ALU.add)
+            nc.sync.dma_start(out[r * P : (r + 1) * P, HALF:J], result[:])

@@ -166,81 +166,94 @@ def tile_attend_bexpectedvalue_kernel(tc, taba, tabb_words, tabb_scales, val, ai
                 scores[1, r].rearrange("p (g k) -> p k g", k=MEMBERS),
             )
             nc.scalar.activation(p0[:, cols[r]], shifted0[:, cols[r]], ACT.Exp)
-            nc.gpsimd.tensor_tensor(pv0[:, cols[r]], p0[:, cols[r]], val_row[:], ALU.mult)
+            width = (HALF, P)[r]
+            share = slice(r * HALF, r * HALF + width)
+            nc.gpsimd.tensor_tensor(pv0[:, share], p0[:, share], val_row[:, 0:width], ALU.mult)
         for r in range(ROW_TILES):
             nc.vector.tensor_reduce(neg_max1[:, groups[r]], by_group(scores[1, r]), AX.X, ALU.max, negate=True)
         neg_max_twice = keep.tile([P, 2, G], F32, name="neg_max_twice")
         nc.scalar.copy(neg_max_twice[:], neg_max1[:].unsqueeze(1).to_broadcast([P, 2, G]))
 
-        turned_ps = bank("turn", "turned_ps")
+        turned_ps = [bank("turn", "turned_ps0"), bank("back", "turned_ps1")]
         for q in range(BLOCKS):
-            turn(block(turned_ps, q), block(dealt1, q), start=(q == 0), stop=False)
+            turn(block(turned_ps[q // 2], q % 2), block(dealt1, q), start=(q % 2 == 0), stop=False)
         for q in range(BLOCKS):
             turn(
-                block(turned_ps, q),
+                block(turned_ps[q // 2], q % 2),
                 neg_max_twice[:].rearrange("p k g -> p (k g)"),
                 start=False,
-                stop=(q == BLOCKS - 1),
+                stop=(q % 2 == 1),
             )
         p_turned = wide("p_turned")
-        nc.scalar.activation(p_turned[:], turned_ps[:], ACT.Exp)
+        for u in range(2):
+            nc.scalar.activation(p_turned[:, cols[u]], turned_ps[u][:, 0:HALF], ACT.Exp)
         pv_turned = wide("pv_turned")
-        for q in range(BLOCKS):
+        for q in range(2, BLOCKS):
             nc.scalar.activation(block(pv_turned, q), block(p_turned, q), ACT.Copy, scale=val_part[:, q : q + 1])
         z_ps = bank("score10", "z_ps")
         for q in range(BLOCKS):
             turn(block(z_ps, 0), block(p_turned, q), start=(q == 0), stop=(q == BLOCKS - 1))
-        n_ps = bank("score11", "n_ps")
-        for q in range(BLOCKS):
-            turn(block(n_ps, 0), block(pv_turned, q), start=(q == 0), stop=(q == BLOCKS - 1))
-        pv1 = bank("pv1", "pv1")
-        for q in range(BLOCKS):
-            turn(block(pv1, q), block(pv_turned, q))
-        p1 = bank("p1", "p1")
-        for q in range(BLOCKS):
-            turn(block(p1, q), block(p_turned, q))
 
         z0 = small("z0")
         rz0 = small("rz0")
-        n0 = small("n0")
+        n0 = pv_turned[:, P - HALF_GROUPS : P + HALF_GROUPS]
         for r in range(ROW_TILES):
             nc.vector.tensor_reduce(z0[:, groups[r]], by_group(p0[:, cols[r]]), AX.X, ALU.add)
         for r in range(ROW_TILES):
             nc.vector.reciprocal(rz0[:, groups[r]], z0[:, groups[r]])
+        nc.vector.tensor_tensor(pv0[:, WIDE - P : WIDE], p0[:, WIDE - P : WIDE], val_row[:, P:HALF], ALU.mult)
         for r in range(ROW_TILES):
             nc.vector.tensor_reduce(n0[:, groups[r]], by_group(pv0[:, cols[r]]), AX.X, ALU.add)
 
         def pair_sum(dst, src_ps):
             nc.vector.tensor_reduce(dst, block(src_ps, 0).rearrange("p (k g) -> p g k", k=2), AX.X, ALU.add)
 
-        def deviation(h, n, rz):
+        def expectation(h, n, rz):
             ev = small(f"ev{h}")
             nc.vector.tensor_tensor(ev[:], n, rz, ALU.mult)
+            return ev
+
+        def deviation(h, ev):
             dev = small(f"dev{h}")
             nc.vector.tensor_tensor(by_row_tile(dev[:]), by_row_tile(ev[:]), aim_sb[:, :, groups[h]], ALU.subtract)
-            return ev, dev
+            return dev
 
-        def factors(h, c, ev, dev, rz):
+        def factor_c(c, dev, rz):
             nc.vector.scalar_tensor_tensor(c, dev[:], 8.0, rz, ALU.mult, ALU.mult)
+
+        def factor_d(h, c, ev):
             d = small(f"d{h}")
             nc.vector.scalar_tensor_tensor(d[:], c, -1.0, ev[:], ALU.mult, ALU.mult)
             return d
 
-        ev0, dev0 = deviation(0, n0[:], rz0[:])
-        z1 = n0
-        pair_sum(z1[:], z_ps)
-        rz1 = small("rz1")
-        nc.vector.reciprocal(rz1[:], z1[:])
+        ev0 = expectation(0, n0, rz0[:])
+        dev0 = deviation(0, ev0)
+        for q in range(2):
+            nc.vector.tensor_scalar_mul(block(pv_turned, q), block(p_turned, q), val_part[:, q : q + 1])
+        n_ps = bank("score11", "n_ps")
+        for q in range(BLOCKS):
+            turn(block(n_ps, 0), block(pv_turned, q), start=(q == 0), stop=(q == BLOCKS - 1))
+        pv1 = bank("pv1", "pv1")
+        for q in range(BLOCKS):
+            turn(block(pv1, q), block(pv_turned, q))
         overlap = keep.tile([P, G + HALF_GROUPS], F32, name="overlap")
         c0 = overlap[:, HALF_GROUPS : HALF_GROUPS + G]
         n1 = overlap[:, 0:G]
-        d0 = factors(0, c0, ev0, dev0, rz0[:])
+        factor_c(c0, dev0, rz0[:])
+        z1 = dev0
+        pair_sum(z1[:], z_ps)
+        p1 = bank("score10", "p1")
+        for q in range(BLOCKS):
+            turn(block(p1, q), block(p_turned, q))
+        d0 = factor_d(0, c0, ev0)
 
         def finish_first_half(r):
             a = keep.tile([P, HALF], F32, name=f"a0{r}")
             b = keep.tile([P, HALF], F32, name=f"b0{r}")
             nc.vector.tensor_tensor(by_group(a[:]), by_group(pv0[:, cols[r]]), spread(c0[:, groups[r]]), ALU.mult)
-            nc.vector.tensor_tensor(by_group(b[:]), by_group(p0[:, cols[r]]), spread(d0[:, groups[r]]), ALU.mult)
+            (nc.gpsimd, nc.vector)[r].tensor_tensor(
+                by_group(b[:]), by_group(p0[:, cols[r]]), spread(d0[:, groups[r]]), ALU.mult
+            )
             sum_ps = bank(f"score0{r}", f"sum_ps{r}")
             terms = (old_sb[:, r, 0:HALF], a[:], b[:])
             for m, term in enumerate(terms):
@@ -256,10 +269,14 @@ def tile_attend_bexpectedvalue_kernel(tc, taba, tabb_words, tabb_scales, val, ai
             nc.scalar.dma_start(out[r * P : (r + 1) * P, 0:HALF], result[:])
 
         finish_first_half(0)
+        rz1 = small("rz1")
+        nc.vector.reciprocal(rz1[:], z1[:])
         pair_sum(n1, n_ps)
-        ev1, dev1 = deviation(1, n1, rz1[:])
+        ev1 = expectation(1, n1, rz1[:])
+        dev1 = deviation(1, ev1)
         c1 = small("c1")
-        d1 = factors(1, c1[:], ev1, dev1, rz1[:])
+        factor_c(c1[:], dev1, rz1[:])
+        d1 = factor_d(1, c1[:], ev1)
         finish_first_half(1)
 
         a1 = wide("a1")

@@ -87,7 +87,7 @@ def tile_attend_bexpectedvalue_kernel(tc, taba, tabb_words, tabb_scales, val, ai
         nc.scalar.copy(
             val_row[:].rearrange("x (p t) -> x p t", t=PACK), val_tp[:, :, 0 : P // 2].rearrange("x t p -> x p t")
         )
-        val_dealt = keep.tile([P, WIDE], F32, name="val_dealt", tag="ahead", align_bytes=64)
+        val_dealt = keep.tile([P, WIDE], F32, name="val_dealt", tag="shared", align_bytes=64)
         for r in range(ROW_TILES):
             nc.scalar.copy(
                 val_dealt[:].rearrange("x (u t r g) -> x r u t g", u=2, t=PACK, r=ROW_TILES)[:, r],
@@ -103,9 +103,13 @@ def tile_attend_bexpectedvalue_kernel(tc, taba, tabb_words, tabb_scales, val, ai
         nc.vector.tensor_copy(b_scale[:], b_scale_all[:].indirect(list_b[:]))
 
         a_grouped = keep.tile([P, I, PACK], BF16, name="a_grouped", tag="shared", align_bytes=64)
-        for t in range(PACK):
+        a_pair = keep.tile([P, 2, I], BF16, name="a_pair")
+        for t in range(2):
+            nc.vector.tensor_copy(a_pair[:, t, :], a_planes[t][:].indirect(list_a[:]))
+        nc.scalar.copy(a_grouped[:, :, 0:2], a_pair[:].rearrange("p t i -> p i t"))
+        for t in range(2, PACK):
             nc.vector.tensor_copy(a_grouped[:, :, t], a_planes[t][:].indirect(list_a[:]))
-        a_codes = keep.tile([P, I], U32, name="a_codes", tag="ahead", align_bytes=64)
+        a_codes = keep.tile([P, I], U32, name="a_codes", align_bytes=64)
         a_scale = keep.tile([P, I], U8, name="a_scale", align_bytes=64)
         nc.vector.quantize_mx(
             out=a_codes[:].bitcast(FP8X4), scales=a_scale[:], in_=a_grouped[:].rearrange("p i t -> p (i t)")

from contextlib import ExitStack

import concourse.mybir as mybir
from concourse.masks import make_identity

D, T, U, I, J, G = 512, 1024, 1024, 256, 512, 64
FLOPS = 2 * D * I * J

F32 = mybir.dt.float32
BF16 = mybir.dt.bfloat16
I32 = mybir.dt.int32
U32 = mybir.dt.uint32
U16 = mybir.dt.uint16
U8 = mybir.dt.uint8
FP8X4 = mybir.dt.float8_e4m3fn_x4
ALU = mybir.AluOpType
ACT = mybir.ActivationFunctionType
AX = mybir.AxisListType

P = 128
PACK = 4
MEMBERS = J // G
ROW_TILES = I // P
HALF = J // 2
HALF_GROUPS = G // 2
WIDE = ROW_TILES * HALF
BLOCKS = WIDE // P


def tile_attend_bexpectedvalue_kernel(tc, taba, tabb_words, tabb_scales, val, aim, old, offs, offs2, out):
    nc = tc.nc
    with ExitStack() as ctx:
        keep = ctx.enter_context(tc.tile_pool(name="keep", bufs=1))
        psum = ctx.enter_context(tc.psum_pool(name="psum", bufs=1))

        def bank(tag, name):
            return psum.tile([P, WIDE], F32, name=name, tag=tag)

        list_a = keep.tile([P, I // 16], U16, name="list_a")
        list_b = keep.tile([P, J // 16], U16, name="list_b")
        nc.sync.dma_start(list_b[:], offs2)
        nc.sync.dma_start(list_a[:], offs)

        val_cols = keep.tile([P, PACK], F32, name="val_cols")
        nc.scalar.dma_start(val_cols[:], val.rearrange("o (p t) -> (o p) t", t=PACK))
        b_scale_all = keep.tile([P, U], U8, name="b_scale_all", align_bytes=64)
        nc.gpsimd.memset(b_scale_all[:].bitcast(I32), 0)
        for q in range(4):
            nc.scalar.dma_start(
                b_scale_all[32 * q : 32 * q + 4, :].bitcast(I32),
                tabb_scales[0, 4 * q : 4 * q + 4, :].bitcast(I32),
            )

        a_rows = taba.rearrange("(p t) c -> p t c", t=PACK)
        a_planes = []
        for t in range(PACK):
            plane = keep.tile([P, T], F32, name=f"a_plane{t}")
            nc.sync.dma_start(plane[:], a_rows[:, t, :])
            a_planes.append(plane)
        b_word_all = keep.tile([P, U], U32, name="b_word_all")
        nc.sync.dma_start(
            b_word_all[:].bitcast(I32),
            tabb_words[0].rearrange("p c r -> p (c r)").bitcast(I32),
        )
        aim_sb = keep.tile([P, ROW_TILES, G], F32, name="aim_sb")
        nc.sync.dma_start(aim_sb[:], aim.rearrange("(r p) g -> p r g", p=P))
        old_sb = keep.tile([P, ROW_TILES, J], F32, name="old_sb")
        nc.sync.dma_start(old_sb[:], old.rearrange("(r p) j -> p r j", p=P))

        ident = keep.tile([P, P], F32, name="ident")
        make_identity(nc, ident[:])

        warm = keep.tile([P, 1], F32, name="warm")
        nc.scalar.activation(warm[:], ident[:, 0:1], ACT.Exp)

        def turn(dst, src, start=True, stop=True):
            nc.tensor.matmul(dst, src, ident[:], start=start, stop=stop, is_transpose=True)

        def block(ap, q):
            return ap[:, q * P : (q + 1) * P]

        val_ps = bank("turn", "val_ps")
        for t in range(PACK):
            turn(block(val_ps, t), val_cols[:, t : t + 1].to_broadcast([P, P]))
        val_tp = val_ps[:].rearrange("x (t p) -> x t p", t=PACK)
        val_row = keep.tile([P, HALF], F32, name="val_row")
        nc.scalar.copy(
            val_row[:].rearrange("x (p t) -> x p t", t=PACK), val_tp[:, :, 0 : P // 2].rearrange("x t p -> x p t")
        )
        val_dealt = keep.tile([P, WIDE], F32, name="val_dealt", tag="shared", align_bytes=64)
        for r in range(ROW_TILES):
            nc.scalar.copy(
                val_dealt[:].rearrange("x (u t r g) -> x r u t g", u=2, t=PACK, r=ROW_TILES)[:, r],
                val_tp[:, :, P // 2 : P].rearrange("x t (g u) -> x u t g", u=2),
            )
        val_ps2 = bank("back", "val_ps2")
        for q in range(BLOCKS):
            turn(block(val_ps2, q), block(val_dealt, q))
        val_part = keep.tile([P, BLOCKS], F32, name="val_part")
        nc.scalar.copy(val_part[:], val_ps2[:].rearrange("x (q c) -> x q c", q=BLOCKS)[:, :, 0])

        b_scale = keep.tile([P, J], U8, name="b_scale", align_bytes=64)
        nc.vector.tensor_copy(b_scale[:], b_scale_all[:].indirect(list_b[:]))

        a_grouped = keep.tile([P, I, PACK], BF16, name="a_grouped", tag="shared", align_bytes=64)
        a_pair = keep.tile([P, 2, I], BF16, name="a_pair")
        for t in range(2):
            nc.vector.tensor_copy(a_pair[:, t, :], a_planes[t][:].indirect(list_a[:]))
        nc.scalar.copy(a_grouped[:, :, 0:2], a_pair[:].rearrange("p t i -> p i t"))
        for t in range(2, PACK):
            nc.vector.tensor_copy(a_grouped[:, :, t], a_planes[t][:].indirect(list_a[:]))
        a_codes = keep.tile([P, I], U32, name="a_codes", align_bytes=64)
        a_scale = keep.tile([P, I], U8, name="a_scale", align_bytes=64)
        nc.vector.quantize_mx(
            out=a_codes[:].bitcast(FP8X4), scales=a_scale[:], in_=a_grouped[:].rearrange("p i t -> p (i t)")
        )

        b_words = keep.tile([P, J], U32, name="b_words", tag="shared", align_bytes=64)
        scores = {}
        for h in range(2):
            nc.vector.tensor_copy(
                b_words[:, h * HALF : (h + 1) * HALF],
                b_word_all[:].indirect(list_b[:, h * (HALF // 16) : (h + 1) * (HALF // 16)]),
            )
            for r in range(ROW_TILES):
                rows = slice(r * P, (r + 1) * P)
                scores[h, r] = bank(f"score{h}{r}", f"score{h}{r}")[:, 0:HALF]
                nc.tensor.matmul_mx(
                    out=scores[h, r],
                    lhsT=a_codes[:, rows].bitcast(FP8X4),
                    lhsT_scale=a_scale[:, rows],
                    rhs=b_words[:, h * HALF : (h + 1) * HALF].bitcast(FP8X4),
                    rhs_scale=b_scale[:, h * HALF : (h + 1) * HALF],
                    start=True,
                    stop=True,
                )

        def by_group(ap):
            return ap.rearrange("p (g k) -> p g k", k=MEMBERS)

        def spread(ap):
            return ap.unsqueeze(2).to_broadcast([P, ap.shape[1], MEMBERS])

        def small(name):
            return keep.tile([P, G], F32, name=name)

        def wide(name):
            return keep.tile([P, WIDE], F32, name=name)

        def by_row_tile(ap):
            return ap.rearrange("p (r g) -> p r g", r=ROW_TILES)

        groups = [slice(r * HALF_GROUPS, (r + 1) * HALF_GROUPS) for r in range(ROW_TILES)]
        cols = [slice(r * HALF, (r + 1) * HALF) for r in range(ROW_TILES)]

        neg_max0 = small("neg_max0")
        neg_max1 = small("neg_max1")
        shifted0 = wide("shifted0")
        p0 = wide("p0")
        pv0 = wide("pv0")
        dealt1 = wide("dealt1")
        for r in range(ROW_TILES):
            nc.vector.tensor_reduce(neg_max0[:, groups[r]], by_group(scores[0, r]), AX.X, ALU.max, negate=True)
        for r in range(ROW_TILES):
            nc.vector.tensor_tensor(
                by_group(shifted0[:, cols[r]]), by_group(scores[0, r]), spread(neg_max0[:, groups[r]]), ALU.add
            )
            nc.scalar.copy(
                dealt1[:].rearrange("p (k g) -> p k g", k=MEMBERS)[:, :, groups[r]],
                scores[1, r].rearrange("p (g k) -> p k g", k=MEMBERS),
            )
            nc.scalar.activation(p0[:, cols[r]], shifted0[:, cols[r]], ACT.Exp)
            width = (HALF, P)[r]
            share = slice(r * HALF, r * HALF + width)
            nc.gpsimd.tensor_tensor(pv0[:, share], p0[:, share], val_row[:, 0:width], ALU.mult)
        for r in range(ROW_TILES):
            nc.vector.tensor_reduce(neg_max1[:, groups[r]], by_group(scores[1, r]), AX.X, ALU.max, negate=True)
        neg_max_twice = keep.tile([P, 2, G], F32, name="neg_max_twice")
        nc.scalar.copy(neg_max_twice[:], neg_max1[:].unsqueeze(1).to_broadcast([P, 2, G]))

        turned_ps = [bank("turn", "turned_ps0"), bank("back", "turned_ps1")]
        for q in range(BLOCKS):
            turn(block(turned_ps[q // 2], q % 2), block(dealt1, q), start=(q % 2 == 0), stop=False)
        for q in range(BLOCKS):
            turn(
                block(turned_ps[q // 2], q % 2),
                neg_max_twice[:].rearrange("p k g -> p (k g)"),
                start=False,
                stop=(q % 2 == 1),
            )
        p_turned = wide("p_turned")
        for u in range(2):
            nc.scalar.activation(p_turned[:, cols[u]], turned_ps[u][:, 0:HALF], ACT.Exp)
        pv_turned = wide("pv_turned")
        for q in range(2, BLOCKS):
            nc.scalar.activation(block(pv_turned, q), block(p_turned, q), ACT.Copy, scale=val_part[:, q : q + 1])
        z_ps = bank("score10", "z_ps")
        for q in range(BLOCKS):
            turn(block(z_ps, 0), block(p_turned, q), start=(q == 0), stop=(q == BLOCKS - 1))

        z0 = small("z0")
        rz0 = small("rz0")
        n0 = pv_turned[:, P - HALF_GROUPS : P + HALF_GROUPS]
        for r in range(ROW_TILES):
            nc.vector.tensor_reduce(z0[:, groups[r]], by_group(p0[:, cols[r]]), AX.X, ALU.add)
        for r in range(ROW_TILES):
            nc.vector.reciprocal(rz0[:, groups[r]], z0[:, groups[r]])
        nc.vector.tensor_tensor(pv0[:, WIDE - P : WIDE], p0[:, WIDE - P : WIDE], val_row[:, P:HALF], ALU.mult)
        for r in range(ROW_TILES):
            nc.vector.tensor_reduce(n0[:, groups[r]], by_group(pv0[:, cols[r]]), AX.X, ALU.add)

        def pair_sum(dst, src_ps):
            nc.vector.tensor_reduce(dst, block(src_ps, 0).rearrange("p (k g) -> p g k", k=2), AX.X, ALU.add)

        def expectation(h, n, rz):
            ev = small(f"ev{h}")
            nc.vector.tensor_tensor(ev[:], n, rz, ALU.mult)
            return ev

        def deviation(h, ev):
            dev = small(f"dev{h}")
            nc.vector.tensor_tensor(by_row_tile(dev[:]), by_row_tile(ev[:]), aim_sb[:, :, groups[h]], ALU.subtract)
            return dev

        def factor_c(c, dev, rz):
            nc.vector.scalar_tensor_tensor(c, dev[:], 8.0, rz, ALU.mult, ALU.mult)

        def factor_d(h, c, ev):
            d = small(f"d{h}")
            nc.vector.scalar_tensor_tensor(d[:], c, -1.0, ev[:], ALU.mult, ALU.mult)
            return d

        ev0 = expectation(0, n0, rz0[:])
        dev0 = deviation(0, ev0)
        for q in range(2):
            nc.vector.tensor_scalar_mul(block(pv_turned, q), block(p_turned, q), val_part[:, q : q + 1])
        n_ps = bank("score11", "n_ps")
        for q in range(BLOCKS):
            turn(block(n_ps, 0), block(pv_turned, q), start=(q == 0), stop=(q == BLOCKS - 1))
        pv1 = bank("pv1", "pv1")
        for q in range(BLOCKS):
            turn(block(pv1, q), block(pv_turned, q))
        overlap = keep.tile([P, G + HALF_GROUPS], F32, name="overlap")
        c0 = overlap[:, HALF_GROUPS : HALF_GROUPS + G]
        n1 = overlap[:, 0:G]
        factor_c(c0, dev0, rz0[:])
        z1 = dev0
        pair_sum(z1[:], z_ps)
        p1 = bank("score10", "p1")
        for q in range(BLOCKS):
            turn(block(p1, q), block(p_turned, q))
        d0 = factor_d(0, c0, ev0)

        def finish_first_half(r):
            a = keep.tile([P, HALF], F32, name=f"a0{r}")
            b = keep.tile([P, HALF], F32, name=f"b0{r}")
            nc.vector.tensor_tensor(by_group(a[:]), by_group(pv0[:, cols[r]]), spread(c0[:, groups[r]]), ALU.mult)
            (nc.gpsimd, nc.vector)[r].tensor_tensor(
                by_group(b[:]), by_group(p0[:, cols[r]]), spread(d0[:, groups[r]]), ALU.mult
            )
            sum_ps = bank(f"score0{r}", f"sum_ps{r}")
            terms = (old_sb[:, r, 0:HALF], a[:], b[:])
            for m, term in enumerate(terms):
                for k in range(HALF // P):
                    turn(block(sum_ps, k), block(term, k), start=(m == 0 and k == 0), stop=(m == 2 and k == 1))
            sum_turned = keep.tile([P, HALF], F32, name=f"sum_turned{r}")
            nc.scalar.copy(sum_turned[:], sum_ps[:, 0:HALF])
            back_ps = bank(("turn", "back")[r], f"back_ps{r}")
            for k in range(HALF // P):
                turn(block(back_ps, k), block(sum_turned, k))
            result = keep.tile([P, HALF], F32, name=f"result0{r}")
            nc.scalar.copy(result[:], back_ps[:, 0:HALF])
            nc.scalar.dma_start(out[r * P : (r + 1) * P, 0:HALF], result[:])

        finish_first_half(0)
        rz1 = small("rz1")
        nc.vector.reciprocal(rz1[:], z1[:])
        pair_sum(n1, n_ps)
        ev1 = expectation(1, n1, rz1[:])
        dev1 = deviation(1, ev1)
        c1 = small("c1")
        factor_c(c1[:], dev1, rz1[:])
        d1 = factor_d(1, c1[:], ev1)
        finish_first_half(1)

        a1 = wide("a1")
        for r in range(ROW_TILES):
            nc.vector.tensor_tensor(
                by_group(a1[:, cols[r]]),
                pv1[:].rearrange("p (k g) -> p g k", k=MEMBERS)[:, groups[r], :],
                spread(c1[:, groups[r]]),
                ALU.mult,
            )
        b1 = wide("b1")
        nc.vector.tensor_tensor(
            by_group(b1[:]), p1[:].rearrange("p (k g) -> p g k", k=MEMBERS), spread(d1[:]), ALU.mult
        )
        partial = [keep.tile([P, HALF], F32, name=f"partial{r}") for r in range(ROW_TILES)]
        for r in range(ROW_TILES):
            (nc.gpsimd, nc.vector)[r].tensor_tensor(partial[r][:], a1[:, cols[r]], old_sb[:, r, HALF:J], ALU.add)
        for r in range(ROW_TILES):
            result = keep.tile([P, HALF], F32, name=f"result1{r}")
            nc.vector.tensor_tensor(result[:], partial[r][:], b1[:, cols[r]], ALU.add)
            nc.sync.dma_start(out[r * P : (r + 1) * P, HALF:J], result[:])
